import numpy as np
import ml_dtypes


def mxq(x, axis, fmt="e4m3"):
    dtype, down = {"e4m3": (ml_dtypes.float8_e4m3fn, 7), "e5m2": (ml_dtypes.float8_e5m2, 14)}[fmt]
    v = np.moveaxis(np.asarray(x, np.float32).astype(ml_dtypes.bfloat16).astype(np.float64), axis, -1)
    blocks = v.reshape(v.shape[:-1] + (-1, 32))
    amax = np.abs(blocks).max(-1, keepdims=True)
    byte = np.maximum(np.where(amax > 0, np.frexp(amax)[1] - 1 + 127, 0) - down, 1)
    scale = np.exp2(byte - 127.0)
    codes = (blocks / scale).astype(np.float32).astype(dtype).astype(np.float64)
    return np.moveaxis((codes * scale).reshape(v.shape), -1, axis)


WIDE = False


def mx_kscale(k):
    if not WIDE:
        return np.ones(k)
    levels = np.array([10, -10, 5, -5, 0])
    if k % 512:
        return np.exp2(np.random.permutation(np.resize(levels, k // 32))).repeat(32)
    a = np.empty((k // 512, 16))
    for p in range(k // 512):
        a[p, :8] = np.random.permutation(np.resize(levels, 8))
        for g in range(8):
            far = levels[np.abs(levels - a[p, g]) >= 10]
            a[p, g + 8] = far[np.random.randint(len(far))]
    return np.exp2(a.ravel()).repeat(32)


BF16 = ml_dtypes.bfloat16


def bf(x):
    return np.asarray(x, np.float32).astype(BF16)


def f64(x):
    return np.asarray(x).astype(np.float64)


E2M1 = np.array([0.0, 0.5, 1.0, 1.5, 2.0, 3.0, 4.0, 6.0, -0.0, -0.5, -1.0, -1.5, -2.0, -3.0, -4.0, -6.0])


def pack_weight(w, fmt):
    k, n = w.shape
    w = f64(bf(w)).reshape(k // 32, 32, n)
    amax = np.abs(w).max(1)
    if fmt == "e4m3":
        byte = np.frexp(amax)[1] - 1 + 127 - 7
    else:
        mant, ex = np.frexp(amax / 6.0)
        byte = np.where(mant > 0.5, ex, ex - 1) + 127
    byte = np.clip(np.where(amax > 0, byte, 1), 1, 254)
    scaled = (w * np.exp2(127.0 - byte)[:, None, :]).reshape(k, n).astype(np.float32)
    by_word = np.ascontiguousarray(scaled.reshape(k // 512, 128, 4, n).transpose(0, 1, 3, 2))
    if fmt == "e4m3":
        words = by_word.astype(ml_dtypes.float8_e4m3fn).view(np.uint8)
    else:
        c = by_word.astype(ml_dtypes.float4_e2m1fn).view(np.uint8) & 0xF
        words = c[..., 0::2] | (c[..., 1::2] << 4)
    return np.ascontiguousarray(words), np.ascontiguousarray(byte.astype(np.uint8).reshape(k // 512, 16, n))


def unpack_weight(words, scales, fmt):
    g, p, n, _ = words.shape
    if fmt == "e4m3":
        vals = np.ascontiguousarray(words).view(ml_dtypes.float8_e4m3fn).astype(np.float64)
    else:
        nib = np.empty((g, p, n, 4), np.uint8)
        nib[..., 0::2] = words & 0xF
        nib[..., 1::2] = words >> 4
        vals = E2M1[nib]
    vals = vals * np.repeat(np.exp2(scales.astype(np.float64) - 127.0), 8, axis=1)[..., None]
    return vals.transpose(0, 1, 3, 2).reshape(g * 512, n)
def pack4(w):
    words, scales = pack_weight(w, "e2m1")
    return words.reshape(words.shape[0], 128, -1), scales


def unpack4(words, scales):
    return unpack_weight(words.reshape(words.shape[0], 128, -1, 2), scales, "e2m1")


def planes(Y):
    n, m = Y.shape
    b = f64(bf(Y)).reshape(n // 32, 32, m)
    amax = np.abs(b).max(1)
    byte = np.clip(np.where(amax > 0, np.frexp(amax)[1] - 1 + 127 - 7, 1), 1, 254)
    codes = (b * np.exp2(127.0 - byte)[:, None, :]).reshape(n, m).astype(np.float32).astype(ml_dtypes.float8_e4m3fn).view(np.uint8)
    words = codes.reshape(n // 512, 128, 4, m).transpose(0, 1, 3, 2)
    return np.ascontiguousarray(words), np.ascontiguousarray(byte.astype(np.uint8).reshape(n // 512, 16, m))


N, B = 2048, 512


def setup_inputs():
    s = mx_kscale(N)
    wt = np.random.randn(N, N) * 0.7 / np.sqrt(N)
    w_words, w_scales = pack4(f64(bf(wt * s[:, None] / s[None, :])))
    t0 = bf(np.random.randn(N, B) / s[:, None])
    t1 = bf(np.random.randn(N, B) / s[:, None])
    rho = bf(np.exp(0.8 * np.random.randn(N)) * s)
    return {"w_words": w_words, "w_scales": w_scales, "t0": t0, "t1": t1, "rho": rho}


def reference(w_words, w_scales, t0, t1, rho):
    W = unpack4(w_words, w_scales)
    T0, T1, r = f64(t0), f64(t1), f64(rho)
    P = W.T @ mxq(T1, 0, "e4m3")
    Z = 2.0 * P - T0
    y = (W.T @ mxq(Z, 0, "e4m3")) * r[:, None]
    Y = y.reshape(N, B)
    words, scales = planes(Y)
    return y, words, scales

@@ -1,0 +1,272 @@
+from contextlib import ExitStack
+
+import concourse.mybir as mybir
+
+N, B = 2048, 512
+FLOPS = 2 * 2 * N * N * B
+
+F32 = mybir.dt.float32
+BF16 = mybir.dt.bfloat16
+I32 = mybir.dt.int32
+U32 = mybir.dt.uint32
+U8 = mybir.dt.uint8
+FP8X4 = mybir.dt.float8_e4m3fn_x4
+FP4X4 = mybir.dt.float4_e2m1fn_x4
+ALU = mybir.AluOpType
+ACT = mybir.ActivationFunctionType
+
+P = 128
+PACK = 4
+GROUP = P * PACK
+GROUPS = N // GROUP
+BANKS = 8
+ALIGN = 256
+
+
+def tile_chebyshev_step_operator_apply_h1_kernel(tc, w_words, w_scales, t0, t1, rho, out_0, out_1, out_2):
+    nc = tc.nc
+    with ExitStack() as ctx:
+        keep = ctx.enter_context(tc.tile_pool(name="keep", bufs=1))
+        rot = ctx.enter_context(tc.tile_pool(name="rot", bufs=4))
+        psum = ctx.enter_context(tc.psum_pool(name="psum", bufs=1))
+        ctx.enter_context(tc.manual_schedule())
+
+        def new(name, shape, dtype):
+            return keep.tile(shape, dtype, name=name, align_bytes=ALIGN)
+
+        s_raw = [new("s_raw%d" % h, [P, GROUPS, 2 * GROUP], U8) for h in range(2)]
+        for h in range(2):
+            nc.vector.memset(s_raw[h][:].rearrange("p g n -> p (g n)").bitcast(I32), 0)
+
+        w_early = [new("w_early%d" % g, [P, 4 * GROUP], U8) for g in range(GROUPS)]
+        w_late = {o: new("w_late%d" % o, [P, GROUPS, 2 * GROUP], U8) for o in (2, 3)}
+        t1_raw = [new("t1_raw%d" % g, [P, PACK, B], BF16) for g in range(GROUPS)]
+        t0_raw = [new("t0_raw%d" % g, [P, PACK, B], BF16) for g in range(GROUPS)]
+        rho_raw = new("rho_raw", [P, GROUPS, PACK], BF16)
+        rho_f32 = new("rho_f32", [P, GROUPS, PACK], F32)
+
+        def load_w_early(g):
+            nc.sync.dma_start(out=w_early[g][:].bitcast(I32), in_=w_words[g][:, 0 : 4 * GROUP].bitcast(I32))
+
+        def load_w_late(o):
+            src = w_words[:, :, 2 * GROUP * o : 2 * GROUP * (o + 1)].bitcast(I32).rearrange("g p n -> p g n")
+            nc.sync.dma_start(out=w_late[o][:].bitcast(I32), in_=src)
+
+        def load_scales(h):
+            for q in range(4):
+                src = w_scales[:, 4 * q : 4 * q + 4, 2 * GROUP * h : 2 * GROUP * (h + 1)].bitcast(I32)
+                nc.sync.dma_start(
+                    out=s_raw[h][32 * q : 32 * q + 4, :, :].bitcast(I32), in_=src.rearrange("g r n -> r g n")
+                )
+
+        def load_rows(dst, src, g):
+            nc.sync.dma_start(out=dst[:], in_=src[GROUP * g : GROUP * (g + 1), :].rearrange("(p t) b -> p t b", t=PACK))
+
+        load_w_early(0)
+        load_rows(t1_raw[0], t1, 0)
+        load_w_early(1)
+        load_scales(0)
+        load_rows(t1_raw[1], t1, 1)
+        for g in (2, 3):
+            load_w_early(g)
+            load_rows(t1_raw[g], t1, g)
+        load_scales(1)
+        load_w_late(2)
+        load_rows(t0_raw[0], t0, 0)
+        load_w_late(3)
+        nc.sync.dma_start(out=rho_raw[:], in_=rho.rearrange("(o p t) -> p o t", p=P, t=PACK))
+        for g in (1, 2, 3):
+            load_rows(t0_raw[g], t0, g)
+
+        w_codes = {}
+        w_plane = {}
+
+        def sort_words_early(g):
+            dst = new("w_sorted_e%d" % g, [P, 4 * GROUP], U8)
+            nc.vector.tensor_copy(
+                out=dst[:].rearrange("p (o t m y) -> p o t m y", o=2, t=PACK, y=2),
+                in_=w_early[g][:].rearrange("p (o m t y) -> p o t m y", o=2, t=PACK, y=2),
+            )
+            for o in range(2):
+                w_codes[g, o] = dst[:, 2 * GROUP * o : 2 * GROUP * (o + 1)]
+
+        def sort_words_late(o, g):
+            dst = new("w_sorted_l%d_%d" % (o, g), [P, 2 * GROUP], U8)
+            nc.vector.tensor_copy(
+                out=dst[:].rearrange("p (t m y) -> p t m y", t=PACK, y=2),
+                in_=w_late[o][:, g, :].rearrange("p (m t y) -> p t m y", t=PACK, y=2),
+            )
+            w_codes[g, o] = dst[:]
+
+        def sort_scales_early(g):
+            dst = new("s_sorted_e%d" % g, [P, 2 * GROUP], U8)
+            nc.vector.tensor_copy(
+                out=dst[:].rearrange("p (o t m) -> p o t m", o=2, t=PACK),
+                in_=s_raw[0][:, g, :].rearrange("p (o m t) -> p o t m", o=2, t=PACK),
+            )
+            for o in range(2):
+                w_plane[g, o] = dst[:, GROUP * o : GROUP * (o + 1)]
+
+        def sort_scales_late(o):
+            dst = new("s_sorted_l%d" % o, [P, GROUPS * GROUP], U8)
+            nc.vector.tensor_copy(
+                out=dst[:].rearrange("p (g t m) -> p g t m", g=GROUPS, t=PACK),
+                in_=s_raw[1][:, :, GROUP * (o - 2) : GROUP * (o - 1)].rearrange("p g (m t) -> p g t m", t=PACK),
+            )
+            for g in range(GROUPS):
+                w_plane[g, o] = dst[:, GROUP * g : GROUP * (g + 1)]
+
+        grouped = {}
+
+        def interleave(key, src, copy, c0=0, c1=B):
+            if key not in grouped:
+                grouped[key] = rot.tile([P, B, PACK], BF16, name="grouped", align_bytes=ALIGN)
+            copy(
+                out=grouped[key][:, c0:c1, :].rearrange("p (c i) t -> p c t i", i=4),
+                in_=src[:, :, c0:c1].rearrange("p t (c i) -> p c t i", i=4),
+            )
+
+        def quantize(key, codes, scales, c0=0, c1=B):
+            nc.vector.quantize_mx(
+                out=codes[:, c0:c1].bitcast(FP8X4),
+                scales=scales[:, c0:c1],
+                in_=grouped[key][:, c0:c1, :].rearrange("p c t -> p (c t)"),
+            )
+
+        operand = {}
+        for name in ("t1", "z"):
+            for g in range(GROUPS):
+                operand[name, g] = (new("%s_codes%d" % (name, g), [P, B], U32), new("%s_plane%d" % (name, g), [P, B], U8))
+
+        def quantize_operand(name, g):
+            codes, plane = operand[name, g]
+            quantize((name, g), codes[:], plane[:])
+
+        acc = {}
+
+        def one_pass(name, o, t, g):
+            if g == 0:
+                acc[name, o, t] = psum.tile([P, B], F32, name="bank%d" % ((PACK * o + t) % BANKS))
+            codes, plane = operand[name, g]
+            nc.tensor.matmul_mx(
+                out=acc[name, o, t][:],
+                lhsT=w_codes[g, o][:, 2 * P * t : 2 * P * (t + 1)].bitcast(FP4X4),
+                lhsT_scale=w_plane[g, o][:, P * t : P * (t + 1)],
+                rhs=codes[:].bitcast(FP8X4),
+                rhs_scale=plane[:],
+                start=(g == 0),
+                stop=(g == GROUPS - 1),
+            )
+
+        def group_pass(name, o, g):
+            for t in range(PACK):
+                one_pass(name, o, t, g)
+
+        def whole_tile(name, o, t):
+            for g in range(GROUPS):
+                one_pass(name, o, t, g)
+
+        z_rows = [new("z_rows%d" % o, [P, PACK, B], BF16) for o in range(GROUPS)]
+
+        def recurrence(o, t):
+            nc.vector.scalar_tensor_tensor(
+                out=z_rows[o][:, t, :], in0=acc["t1", o, t][:], scalar=2.0, in1=t0_raw[o][:, t, :],
+                op0=ALU.mult, op1=ALU.subtract,
+            )
+
+        def t1_step(g):
+            quantize_operand("t1", g)
+            group_pass("t1", 0, g)
+            group_pass("t1", 1, g)
+
+        for g in range(GROUPS):
+            interleave(("t1", g), t1_raw[g], nc.scalar.copy)
+        nc.scalar.activation(out=rho_f32[:], in_=rho_raw[:], func=ACT.Copy)
+
+        sort_words_early(0)
+        sort_words_early(1)
+        sort_scales_early(0)
+        sort_scales_early(1)
+        t1_step(0)
+        sort_scales_early(2)
+        sort_scales_early(3)
+        sort_words_early(2)
+        t1_step(1)
+        sort_words_early(3)
+        t1_step(2)
+        sort_scales_late(2)
+        sort_words_late(2, 0)
+        sort_words_late(2, 1)
+        t1_step(3)
+        sort_words_late(2, 2)
+        sort_words_late(2, 3)
+
+        for t in range(PACK):
+            recurrence(0, t)
+            whole_tile("t1", 2, t)
+        interleave(("z", 0), z_rows[0], nc.scalar.copy)
+        sort_scales_late(3)
+        for g in range(GROUPS):
+            sort_words_late(3, g)
+        for t in range(PACK):
+            recurrence(1, t)
+            whole_tile("t1", 3, t)
+        interleave(("z", 1), z_rows[1], nc.scalar.copy)
+        quantize_operand("z", 0)
+        for t in range(PACK):
+            recurrence(2, t)
+        interleave(("z", 2), z_rows[2], nc.scalar.copy)
+        group_pass("z", 0, 0)
+        quantize_operand("z", 1)
+        group_pass("z", 0, 1)
+        for t in range(PACK):
+            recurrence(3, t)
+        interleave(("z", 3), z_rows[3], nc.scalar.copy)
+        group_pass("z", 1, 0)
+        group_pass("z", 1, 1)
+        for g in (2, 3):
+            quantize_operand("z", g)
+            group_pass("z", 0, g)
+            group_pass("z", 1, g)
+
+        y_rows = [new("y_rows%d" % o, [P, PACK, B], F32) for o in range(GROUPS)]
+        y_codes = [new("y_codes%d" % o, [P, B], U32) for o in range(GROUPS)]
+        y_planes = new("y_planes", [P, B], U8)
+
+        def weigh(o, t, c0=0, c1=B):
+            nc.scalar.activation(
+                out=y_rows[o][:, t, c0:c1], in_=acc["z", o, t][:, c0:c1], func=ACT.Copy, scale=rho_f32[:, o, t : t + 1]
+            )
+
+        def out_rows(o):
+            return out_0[GROUP * o : GROUP * (o + 1), :].rearrange("(p t) b -> p t b", t=PACK)
+
+        def store_codes(o):
+            nc.sync.dma_start(out=out_1[o].rearrange("p m t -> p (m t)").bitcast(I32), in_=y_codes[o][:].bitcast(I32))
+
+        last = GROUPS - 1
+        for o in range(last):
+            for t in range(PACK):
+                weigh(o, t)
+                if o + 2 < GROUPS:
+                    whole_tile("z", o + 2, t)
+            nc.sync.dma_start(out=out_rows(o), in_=y_rows[o][:])
+            interleave(("y", o), y_rows[o], nc.vector.tensor_copy)
+            quantize(("y", o), y_codes[o][:], y_planes[4 * o :, :])
+            store_codes(o)
+        halves = [(0, B // 2), (B // 2, B)]
+        for t in range(PACK - 1):
+            weigh(last, t)
+            nc.sync.dma_start(out=out_rows(last)[:, t, :], in_=y_rows[last][:, t, :])
+        for c0, c1 in halves:
+            weigh(last, PACK - 1, c0, c1)
+            interleave(("y", last), y_rows[last], nc.vector.tensor_copy, c0, c1)
+        nc.sync.dma_start(out=out_rows(last)[:, PACK - 1, :], in_=y_rows[last][:, PACK - 1, :])
+        for c0, c1 in halves:
+            quantize(("y", last), y_codes[last][:], y_planes[4 * last :, :], c0, c1)
+        store_codes(last)
+        for q in range(4):
+            queue = nc.scalar if q % 2 == 0 else nc.sync
+            queue.dma_start(
+                out=out_2[:, 4 * q : 4 * q + 4, :].bitcast(I32), in_=y_planes[32 * q : 32 * q + 16, :].bitcast(I32)
+            )

@@ -21,6 +21,7 @@ GROUP = P * PACK
 GROUPS = N // GROUP
 BANKS = 8
 ALIGN = 256
+SPLIT = 192
 
 
 def tile_chebyshev_step_operator_apply_h1_kernel(tc, w_words, w_scales, t0, t1, rho, out_0, out_1, out_2):
@@ -34,9 +35,11 @@ def tile_chebyshev_step_operator_apply_h1_kernel(tc, w_words, w_scales, t0, t1, 
         def new(name, shape, dtype):
             return keep.tile(shape, dtype, name=name, align_bytes=ALIGN)
 
-        s_raw = [new("s_raw%d" % h, [P, GROUPS, 2 * GROUP], U8) for h in range(2)]
-        for h in range(2):
-            nc.vector.memset(s_raw[h][:].rearrange("p g n -> p (g n)").bitcast(I32), 0)
+        s_raw = new("s_raw", [P, N], U8)
+        s_sorted = [new("s_sorted%d" % g, [P, N], U8) for g in range(GROUPS)]
+        nc.vector.memset(s_raw[:].bitcast(I32), 0)
+        for g in range(1, GROUPS):
+            nc.vector.memset(s_sorted[g][:].bitcast(I32), 0)
 
         w_early = [new("w_early%d" % g, [P, 4 * GROUP], U8) for g in range(GROUPS)]
         w_late = {o: new("w_late%d" % o, [P, GROUPS, 2 * GROUP], U8) for o in (2, 3)}
@@ -52,69 +55,38 @@ def tile_chebyshev_step_operator_apply_h1_kernel(tc, w_words, w_scales, t0, t1, 
             src = w_words[:, :, 2 * GROUP * o : 2 * GROUP * (o + 1)].bitcast(I32).rearrange("g p n -> p g n")
             nc.sync.dma_start(out=w_late[o][:].bitcast(I32), in_=src)
 
-        def load_scales(h):
+        def load_scales():
             for q in range(4):
-                src = w_scales[:, 4 * q : 4 * q + 4, 2 * GROUP * h : 2 * GROUP * (h + 1)].bitcast(I32)
                 nc.sync.dma_start(
-                    out=s_raw[h][32 * q : 32 * q + 4, :, :].bitcast(I32), in_=src.rearrange("g r n -> r g n")
+                    out=s_raw[32 * q : 32 * q + 16, :].bitcast(I32), in_=w_scales[:, 4 * q : 4 * q + 4, :].bitcast(I32)
                 )
+
+        def move_scales(g):
+            for r in range(4):
+                nc.sync.dma_start(
+                    out=s_sorted[g][r:P:32, :].bitcast(I32), in_=s_sorted[0][4 * g + r : P : 32, :].bitcast(I32)
+                )
+
+        def sort_scales():
+            nc.vector.tensor_copy(
+                out=s_sorted[0][:].rearrange("p (o t m) -> p o t m", o=GROUPS, t=PACK),
+                in_=s_raw[:].rearrange("p (o m t) -> p o t m", o=GROUPS, t=PACK),
+            )
 
         def load_rows(dst, src, g):
             nc.sync.dma_start(out=dst[:], in_=src[GROUP * g : GROUP * (g + 1), :].rearrange("(p t) b -> p t b", t=PACK))
 
-        load_w_early(0)
-        load_rows(t1_raw[0], t1, 0)
-        load_w_early(1)
-        load_scales(0)
-        load_rows(t1_raw[1], t1, 1)
-        for g in (2, 3):
-            load_w_early(g)
-            load_rows(t1_raw[g], t1, g)
-        load_scales(1)
-        load_w_late(2)
-        load_rows(t0_raw[0], t0, 0)
-        load_w_late(3)
-        nc.sync.dma_start(out=rho_raw[:], in_=rho.rearrange("(o p t) -> p o t", p=P, t=PACK))
-        for g in (1, 2, 3):
-            load_rows(t0_raw[g], t0, g)
-
         w_codes = {}
-        w_plane = {}
+        w_plane = {(g, o): s_sorted[g][:, GROUP * o : GROUP * (o + 1)] for g in range(GROUPS) for o in range(GROUPS)}
 
-        def sort_words_early(g):
-            dst = new("w_sorted_e%d" % g, [P, 4 * GROUP], U8)
-            nc.vector.tensor_copy(
-                out=dst[:].rearrange("p (o t m y) -> p o t m y", o=2, t=PACK, y=2),
-                in_=w_early[g][:].rearrange("p (o m t y) -> p o t m y", o=2, t=PACK, y=2),
-            )
-            for o in range(2):
-                w_codes[g, o] = dst[:, 2 * GROUP * o : 2 * GROUP * (o + 1)]
-
-        def sort_words_late(o, g):
-            dst = new("w_sorted_l%d_%d" % (o, g), [P, 2 * GROUP], U8)
+        def sort_words(g, o):
+            src = w_early[g][:, 2 * GROUP * o : 2 * GROUP * (o + 1)] if o < 2 else w_late[o][:, g, :]
+            dst = new("w_sorted%d_%d" % (o, g), [P, 2 * GROUP], U8)
             nc.vector.tensor_copy(
                 out=dst[:].rearrange("p (t m y) -> p t m y", t=PACK, y=2),
-                in_=w_late[o][:, g, :].rearrange("p (m t y) -> p t m y", t=PACK, y=2),
+                in_=src.rearrange("p (m t y) -> p t m y", t=PACK, y=2),
             )
             w_codes[g, o] = dst[:]
-
-        def sort_scales_early(g):
-            dst = new("s_sorted_e%d" % g, [P, 2 * GROUP], U8)
-            nc.vector.tensor_copy(
-                out=dst[:].rearrange("p (o t m) -> p o t m", o=2, t=PACK),
-                in_=s_raw[0][:, g, :].rearrange("p (o m t) -> p o t m", o=2, t=PACK),
-            )
-            for o in range(2):
-                w_plane[g, o] = dst[:, GROUP * o : GROUP * (o + 1)]
-
-        def sort_scales_late(o):
-            dst = new("s_sorted_l%d" % o, [P, GROUPS * GROUP], U8)
-            nc.vector.tensor_copy(
-                out=dst[:].rearrange("p (g t m) -> p g t m", g=GROUPS, t=PACK),
-                in_=s_raw[1][:, :, GROUP * (o - 2) : GROUP * (o - 1)].rearrange("p g (m t) -> p g t m", t=PACK),
-            )
-            for g in range(GROUPS):
-                w_plane[g, o] = dst[:, GROUP * g : GROUP * (g + 1)]
 
         grouped = {}
 
@@ -174,40 +146,52 @@ def tile_chebyshev_step_operator_apply_h1_kernel(tc, w_words, w_scales, t0, t1, 
                 op0=ALU.mult, op1=ALU.subtract,
             )
 
-        def t1_step(g):
-            quantize_operand("t1", g)
-            group_pass("t1", 0, g)
-            group_pass("t1", 1, g)
+        load_w_early(0)
+        load_scales()
+        load_rows(t1_raw[0], t1, 0)
+        load_rows(t1_raw[1], t1, 1)
+        load_w_early(1)
+        load_rows(t1_raw[2], t1, 2)
+        sort_words(0, 0)
+        sort_scales()
+        move_scales(1)
+        load_w_early(2)
+        load_rows(t1_raw[3], t1, 3)
+        move_scales(2)
+        load_w_early(3)
+        move_scales(3)
+        load_w_late(2)
+        load_rows(t0_raw[0], t0, 0)
+        load_w_late(3)
+        nc.sync.dma_start(out=rho_raw[:], in_=rho.rearrange("(o p t) -> p o t", p=P, t=PACK))
+        for g in (1, 2, 3):
+            load_rows(t0_raw[g], t0, g)
 
-        for g in range(GROUPS):
+        interleave(("t1", 0), t1_raw[0], nc.scalar.copy, 0, SPLIT)
+        for g in range(1, GROUPS):
             interleave(("t1", g), t1_raw[g], nc.scalar.copy)
         nc.scalar.activation(out=rho_f32[:], in_=rho_raw[:], func=ACT.Copy)
 
-        sort_words_early(0)
-        sort_words_early(1)
-        sort_scales_early(0)
-        sort_scales_early(1)
-        t1_step(0)
-        sort_scales_early(2)
-        sort_scales_early(3)
-        sort_words_early(2)
-        t1_step(1)
-        sort_words_early(3)
-        t1_step(2)
-        sort_scales_late(2)
-        sort_words_late(2, 0)
-        sort_words_late(2, 1)
-        t1_step(3)
-        sort_words_late(2, 2)
-        sort_words_late(2, 3)
+        interleave(("t1", 0), t1_raw[0], nc.vector.tensor_copy, SPLIT, B)
+        quantize_operand("t1", 0)
+        sort_words(0, 1)
+        group_pass("t1", 0, 0)
+        group_pass("t1", 1, 0)
+        for g in range(1, GROUPS):
+            sort_words(g, 0)
+            sort_words(g, 1)
+            quantize_operand("t1", g)
+            group_pass("t1", 0, g)
+            group_pass("t1", 1, g)
+        for g in range(GROUPS):
+            sort_words(g, 2)
 
         for t in range(PACK):
             recurrence(0, t)
             whole_tile("t1", 2, t)
         interleave(("z", 0), z_rows[0], nc.scalar.copy)
-        sort_scales_late(3)
         for g in range(GROUPS):
-            sort_words_late(3, g)
+            sort_words(g, 3)
         for t in range(PACK):
             recurrence(1, t)
             whole_tile("t1", 3, t)
@@ -241,30 +225,58 @@ def tile_chebyshev_step_operator_apply_h1_kernel(tc, w_words, w_scales, t0, t1, 
         def out_rows(o):
             return out_0[GROUP * o : GROUP * (o + 1), :].rearrange("(p t) b -> p t b", t=PACK)
 
-        def store_codes(o):
-            nc.sync.dma_start(out=out_1[o].rearrange("p m t -> p (m t)").bitcast(I32), in_=y_codes[o][:].bitcast(I32))
+        def store_codes(o, c0, c1):
+            nc.sync.dma_start(
+                out=out_1[o].rearrange("p m t -> p (m t)").bitcast(I32)[:, c0:c1], in_=y_codes[o][:, c0:c1].bitcast(I32)
+            )
 
         last = GROUPS - 1
+        chunks = [(c0, c0 + P) for c0 in range(0, B, P)]
+        chunk_acc = []
+
+        def last_tile():
+            for c, (c0, c1) in enumerate(chunks):
+                bank = psum.tile([P, P], F32, name="bank%d" % ((BANKS - 1 + c) % BANKS))
+                chunk_acc.append(bank)
+                for g in range(GROUPS):
+                    codes, plane = operand["z", g]
+                    nc.tensor.matmul_mx(
+                        out=bank[:],
+                        lhsT=w_codes[g, last][:, 2 * P * (PACK - 1) :].bitcast(FP4X4),
+                        lhsT_scale=w_plane[g, last][:, P * (PACK - 1) :],
+                        rhs=codes[:, c0:c1].bitcast(FP8X4),
+                        rhs_scale=plane[:, c0:c1],
+                        start=(g == 0),
+                        stop=(g == GROUPS - 1),
+                    )
+
         for o in range(last):
             for t in range(PACK):
                 weigh(o, t)
-                if o + 2 < GROUPS:
+                if o + 2 < GROUPS and (o + 2, t) != (last, PACK - 1):
                     whole_tile("z", o + 2, t)
             nc.sync.dma_start(out=out_rows(o), in_=y_rows[o][:])
             interleave(("y", o), y_rows[o], nc.vector.tensor_copy)
             quantize(("y", o), y_codes[o][:], y_planes[4 * o :, :])
-            store_codes(o)
-        halves = [(0, B // 2), (B // 2, B)]
+            store_codes(o, 0, B)
+        last_tile()
         for t in range(PACK - 1):
             weigh(last, t)
-            nc.sync.dma_start(out=out_rows(last)[:, t, :], in_=y_rows[last][:, t, :])
-        for c0, c1 in halves:
-            weigh(last, PACK - 1, c0, c1)
-            interleave(("y", last), y_rows[last], nc.vector.tensor_copy, c0, c1)
-        nc.sync.dma_start(out=out_rows(last)[:, PACK - 1, :], in_=y_rows[last][:, PACK - 1, :])
-        for c0, c1 in halves:
-            quantize(("y", last), y_codes[last][:], y_planes[4 * last :, :], c0, c1)
-        store_codes(last)
+            if t > 0:
+                t_from = 0 if t == 1 else t
+                nc.sync.dma_start(out=out_rows(last)[:, t_from : t + 1, :], in_=y_rows[last][:, t_from : t + 1, :])
+        for c, (c0, c1) in enumerate(chunks):
+            nc.scalar.activation(
+                out=y_rows[last][:, PACK - 1, c0:c1], in_=chunk_acc[c][:], func=ACT.Copy,
+                scale=rho_f32[:, last, PACK - 1 : PACK],
+            )
+            if c == len(chunks) - 1:
+                nc.sync.dma_start(out=out_rows(last)[:, PACK - 1, :], in_=y_rows[last][:, PACK - 1, :])
+            interleave(("y", last), y_rows[last], nc.scalar.copy if c == len(chunks) - 1 else nc.vector.tensor_copy, c0, c1)
+            if c > 0:
+                quantize(("y", last), y_codes[last][:], y_planes[4 * last :, :], c0 - P, c0)
+        quantize(("y", last), y_codes[last][:], y_planes[4 * last :, :], B - P, B)
+        store_codes(last, 0, B)
         for q in range(4):
             queue = nc.scalar if q % 2 == 0 else nc.sync
             queue.dma_start(

@@ -16,268 +16,271 @@ ALU = mybir.AluOpType
 ACT = mybir.ActivationFunctionType
 
 P = 128
-PACK = 4
-GROUP = P * PACK
+SLOTS = 4
+GROUP = P * SLOTS
 GROUPS = N // GROUP
 BANKS = 8
+WORD = 2
+QUADS = 4
 ALIGN = 256
-SPLIT = 192
+EARLY = BANKS // SLOTS
+SCALAR_FIRST_T1 = 192
+SCALAR_LAST_Z = 256
 
 
 def tile_chebyshev_step_operator_apply_h1_kernel(tc, w_words, w_scales, t0, t1, rho, out_0, out_1, out_2):
     nc = tc.nc
     with ExitStack() as ctx:
         keep = ctx.enter_context(tc.tile_pool(name="keep", bufs=1))
-        rot = ctx.enter_context(tc.tile_pool(name="rot", bufs=4))
+        staging = ctx.enter_context(tc.tile_pool(name="staging", bufs=GROUPS))
         psum = ctx.enter_context(tc.psum_pool(name="psum", bufs=1))
         ctx.enter_context(tc.manual_schedule())
 
         def new(name, shape, dtype):
             return keep.tile(shape, dtype, name=name, align_bytes=ALIGN)
 
-        s_raw = new("s_raw", [P, N], U8)
-        s_sorted = [new("s_sorted%d" % g, [P, N], U8) for g in range(GROUPS)]
-        nc.vector.memset(s_raw[:].bitcast(I32), 0)
-        for g in range(1, GROUPS):
-            nc.vector.memset(s_sorted[g][:].bitcast(I32), 0)
-
-        w_early = [new("w_early%d" % g, [P, 4 * GROUP], U8) for g in range(GROUPS)]
-        w_late = {o: new("w_late%d" % o, [P, GROUPS, 2 * GROUP], U8) for o in (2, 3)}
-        t1_raw = [new("t1_raw%d" % g, [P, PACK, B], BF16) for g in range(GROUPS)]
-        t0_raw = [new("t0_raw%d" % g, [P, PACK, B], BF16) for g in range(GROUPS)]
-        rho_raw = new("rho_raw", [P, GROUPS, PACK], BF16)
-        rho_f32 = new("rho_f32", [P, GROUPS, PACK], F32)
-
-        def load_w_early(g):
-            nc.sync.dma_start(out=w_early[g][:].bitcast(I32), in_=w_words[g][:, 0 : 4 * GROUP].bitcast(I32))
-
-        def load_w_late(o):
-            src = w_words[:, :, 2 * GROUP * o : 2 * GROUP * (o + 1)].bitcast(I32).rearrange("g p n -> p g n")
-            nc.sync.dma_start(out=w_late[o][:].bitcast(I32), in_=src)
+        scales_raw = new("scales_raw", [P, N], U8)
+        w_plane = [new("w_plane%d" % g, [P, N], U8) for g in range(GROUPS)]
+        for tile in [scales_raw] + w_plane[1:]:
+            nc.vector.memset(tile[:].bitcast(I32), 0)
 
         def load_scales():
-            for q in range(4):
+            for q in (0, 2, 1, 3):
                 nc.sync.dma_start(
-                    out=s_raw[32 * q : 32 * q + 16, :].bitcast(I32), in_=w_scales[:, 4 * q : 4 * q + 4, :].bitcast(I32)
-                )
-
-        def move_scales(g):
-            for r in range(4):
-                nc.sync.dma_start(
-                    out=s_sorted[g][r:P:32, :].bitcast(I32), in_=s_sorted[0][4 * g + r : P : 32, :].bitcast(I32)
+                    out=scales_raw[32 * q : 32 * q + 16, :].bitcast(I32),
+                    in_=w_scales[:, 4 * q : 4 * q + 4, :].bitcast(I32),
                 )
 
         def sort_scales():
             nc.vector.tensor_copy(
-                out=s_sorted[0][:].rearrange("p (o t m) -> p o t m", o=GROUPS, t=PACK),
-                in_=s_raw[:].rearrange("p (o m t) -> p o t m", o=GROUPS, t=PACK),
+                out=w_plane[0][:].rearrange("p (o t m) -> p o t m", o=GROUPS, t=SLOTS),
+                in_=scales_raw[:].rearrange("p (o m t) -> p o t m", o=GROUPS, t=SLOTS),
             )
 
-        def load_rows(dst, src, g):
-            nc.sync.dma_start(out=dst[:], in_=src[GROUP * g : GROUP * (g + 1), :].rearrange("(p t) b -> p t b", t=PACK))
+        def move_scales(g):
+            for r in range(4):
+                nc.sync.dma_start(
+                    out=w_plane[g][r:P:32, :].bitcast(I32), in_=w_plane[0][4 * g + r : P : 32, :].bitcast(I32)
+                )
 
-        w_codes = {}
-        w_plane = {(g, o): s_sorted[g][:, GROUP * o : GROUP * (o + 1)] for g in range(GROUPS) for o in range(GROUPS)}
+        w_early = [new("w_early%d" % g, [P, EARLY * GROUP * WORD], U8) for g in range(GROUPS)]
+        w_late = {o: new("w_late%d" % o, [P, GROUPS, GROUP * WORD], U8) for o in range(EARLY, GROUPS)}
+        w_tile = {}
 
-        def sort_words(g, o):
-            src = w_early[g][:, 2 * GROUP * o : 2 * GROUP * (o + 1)] if o < 2 else w_late[o][:, g, :]
-            dst = new("w_sorted%d_%d" % (o, g), [P, 2 * GROUP], U8)
+        def load_w_early(g):
+            nc.sync.dma_start(out=w_early[g][:].bitcast(I32), in_=w_words[g][:, 0 : EARLY * GROUP * WORD].bitcast(I32))
+
+        def load_w_late(o):
+            columns = w_words[:, :, GROUP * WORD * o : GROUP * WORD * (o + 1)]
+            nc.sync.dma_start(out=w_late[o][:].bitcast(I32), in_=columns.bitcast(I32).rearrange("g p n -> p g n"))
+
+        def sort_words_of_pass(g, o):
+            dst = new("w_pass%d_%d" % (g, o), [P, GROUP * WORD], U8)
+            src = w_early[g][:, GROUP * WORD * o : GROUP * WORD * (o + 1)]
             nc.vector.tensor_copy(
-                out=dst[:].rearrange("p (t m y) -> p t m y", t=PACK, y=2),
-                in_=src.rearrange("p (m t y) -> p t m y", t=PACK, y=2),
+                out=dst[:].rearrange("p (t m y) -> p t m y", t=SLOTS, y=WORD),
+                in_=src.rearrange("p (m t y) -> p t m y", t=SLOTS, y=WORD),
             )
-            w_codes[g, o] = dst[:]
+            for t in range(SLOTS):
+                w_tile[g, o, t] = dst[:, P * WORD * t : P * WORD * (t + 1)]
 
-        grouped = {}
+        def sort_words_of_slot(o, t):
+            dst = new("w_slot%d_%d" % (o, t), [P, GROUPS, P * WORD], U8)
+            nc.vector.tensor_copy(
+                out=dst[:].rearrange("p g (m y) -> p g m y", y=WORD),
+                in_=w_late[o][:].rearrange("p g (m t y) -> p g m t y", t=SLOTS, y=WORD)[:, :, :, t, :],
+            )
+            for g in range(GROUPS):
+                w_tile[g, o, t] = dst[:, g, :]
 
-        def interleave(key, src, copy, c0=0, c1=B):
-            if key not in grouped:
-                grouped[key] = rot.tile([P, B, PACK], BF16, name="grouped", align_bytes=ALIGN)
+        t1_rows = [new("t1_rows%d" % g, [P, SLOTS, B], BF16) for g in range(GROUPS)]
+        t0_rows = [new("t0_rows%d" % g, [P, SLOTS, B], BF16) for g in range(GROUPS)]
+        z_rows = [new("z_rows%d" % g, [P, SLOTS, B], BF16) for g in range(GROUPS)]
+        y_rows = [new("y_rows%d" % g, [P, SLOTS, B], F32) for g in range(GROUPS)]
+        rho_bf16 = new("rho_bf16", [P, GROUPS, SLOTS], BF16)
+        rho_f32 = new("rho_f32", [P, GROUPS, SLOTS], F32)
+
+        def group_rows(matrix, g):
+            return matrix[GROUP * g : GROUP * (g + 1), :].rearrange("(p t) b -> p t b", t=SLOTS)
+
+        def load_rows(tiles, matrix, g):
+            nc.sync.dma_start(out=tiles[g][:], in_=group_rows(matrix, g))
+
+        interleaved = {}
+
+        def interleave(name, rows, g, copy, c0=0, c1=B):
+            if (name, g) not in interleaved:
+                interleaved[name, g] = staging.tile([P, B, SLOTS], BF16, name="interleaved", align_bytes=ALIGN)
             copy(
-                out=grouped[key][:, c0:c1, :].rearrange("p (c i) t -> p c t i", i=4),
-                in_=src[:, :, c0:c1].rearrange("p t (c i) -> p c t i", i=4),
+                out=interleaved[name, g][:, c0:c1, :].rearrange("p (c i) t -> p c t i", i=4),
+                in_=rows[g][:, :, c0:c1].rearrange("p t (c i) -> p c t i", i=4),
             )
 
-        def quantize(key, codes, scales, c0=0, c1=B):
-            nc.vector.quantize_mx(
-                out=codes[:, c0:c1].bitcast(FP8X4),
-                scales=scales[:, c0:c1],
-                in_=grouped[key][:, c0:c1, :].rearrange("p c t -> p (c t)"),
-            )
-
-        operand = {}
+        codes, plane = {}, {}
         for name in ("t1", "z"):
             for g in range(GROUPS):
-                operand[name, g] = (new("%s_codes%d" % (name, g), [P, B], U32), new("%s_plane%d" % (name, g), [P, B], U8))
+                codes[name, g] = new("%s_codes%d" % (name, g), [P, B], U32)
+                plane[name, g] = new("%s_plane%d" % (name, g), [P, B], U8)[:]
+        y_planes = new("y_planes", [P, B], U8)
+        for g in range(GROUPS):
+            codes["y", g] = new("y_codes%d" % g, [P, B], U32)
+            plane["y", g] = y_planes[4 * g :, :]
 
-        def quantize_operand(name, g):
-            codes, plane = operand[name, g]
-            quantize((name, g), codes[:], plane[:])
+        def quantize(name, g, c0=0, c1=B):
+            nc.vector.quantize_mx(
+                out=codes[name, g][:, c0:c1].bitcast(FP8X4),
+                scales=plane[name, g][:, c0:c1],
+                in_=interleaved[name, g][:, c0:c1, :].rearrange("p c t -> p (c t)"),
+            )
 
-        acc = {}
+        sums = {}
 
-        def one_pass(name, o, t, g):
-            if g == 0:
-                acc[name, o, t] = psum.tile([P, B], F32, name="bank%d" % ((PACK * o + t) % BANKS))
-            codes, plane = operand[name, g]
+        def bank_tile(bank, columns):
+            return psum.tile([P, columns], F32, name="bank%d" % (bank % BANKS))
+
+        def one_pass(dst, name, o, t, g, c0=0, c1=B):
             nc.tensor.matmul_mx(
-                out=acc[name, o, t][:],
-                lhsT=w_codes[g, o][:, 2 * P * t : 2 * P * (t + 1)].bitcast(FP4X4),
-                lhsT_scale=w_plane[g, o][:, P * t : P * (t + 1)],
-                rhs=codes[:].bitcast(FP8X4),
-                rhs_scale=plane[:],
+                out=dst[:],
+                lhsT=w_tile[g, o, t].bitcast(FP4X4),
+                lhsT_scale=w_plane[g][:, GROUP * o + P * t : GROUP * o + P * (t + 1)],
+                rhs=codes[name, g][:, c0:c1].bitcast(FP8X4),
+                rhs_scale=plane[name, g][:, c0:c1],
                 start=(g == 0),
                 stop=(g == GROUPS - 1),
             )
 
         def group_pass(name, o, g):
-            for t in range(PACK):
-                one_pass(name, o, t, g)
+            for t in range(SLOTS):
+                if g == 0:
+                    sums[name, o, t] = bank_tile(SLOTS * o + t, B)
+                one_pass(sums[name, o, t], name, o, t, g)
 
         def whole_tile(name, o, t):
+            sums[name, o, t] = bank_tile(SLOTS * o + t, B)
             for g in range(GROUPS):
-                one_pass(name, o, t, g)
-
-        z_rows = [new("z_rows%d" % o, [P, PACK, B], BF16) for o in range(GROUPS)]
+                one_pass(sums[name, o, t], name, o, t, g)
 
         def recurrence(o, t):
             nc.vector.scalar_tensor_tensor(
-                out=z_rows[o][:, t, :], in0=acc["t1", o, t][:], scalar=2.0, in1=t0_raw[o][:, t, :],
+                out=z_rows[o][:, t, :], in0=sums["t1", o, t][:], scalar=2.0, in1=t0_rows[o][:, t, :],
                 op0=ALU.mult, op1=ALU.subtract,
             )
 
+        def weigh(src, o, t, c0=0, c1=B):
+            nc.scalar.activation(out=y_rows[o][:, t, c0:c1], in_=src[:], func=ACT.Copy, scale=rho_f32[:, o, t : t + 1])
+
+        def store_rows(o, t):
+            nc.sync.dma_start(out=group_rows(out_0, o)[:, t, :], in_=y_rows[o][:, t, :])
+
+        def store_codes(o):
+            nc.sync.dma_start(out=out_1[o].rearrange("p m t -> p (m t)").bitcast(I32), in_=codes["y", o][:].bitcast(I32))
+
         load_w_early(0)
         load_scales()
-        load_rows(t1_raw[0], t1, 0)
-        load_rows(t1_raw[1], t1, 1)
+        load_rows(t1_rows, t1, 0)
+        load_rows(t1_rows, t1, 1)
         load_w_early(1)
-        load_rows(t1_raw[2], t1, 2)
-        sort_words(0, 0)
+        load_rows(t1_rows, t1, 2)
+        load_w_early(2)
+        sort_words_of_pass(0, 0)
         sort_scales()
         move_scales(1)
-        load_w_early(2)
-        load_rows(t1_raw[3], t1, 3)
-        move_scales(2)
+        load_rows(t1_rows, t1, 3)
         load_w_early(3)
-        move_scales(3)
+        move_scales(2)
         load_w_late(2)
-        load_rows(t0_raw[0], t0, 0)
+        move_scales(3)
+        load_rows(t0_rows, t0, 0)
         load_w_late(3)
-        nc.sync.dma_start(out=rho_raw[:], in_=rho.rearrange("(o p t) -> p o t", p=P, t=PACK))
-        for g in (1, 2, 3):
-            load_rows(t0_raw[g], t0, g)
+        load_rows(t0_rows, t0, 1)
+        nc.sync.dma_start(out=rho_bf16[:], in_=rho.rearrange("(g p t) -> p g t", p=P, t=SLOTS))
+        load_rows(t0_rows, t0, 2)
+        load_rows(t0_rows, t0, 3)
 
-        interleave(("t1", 0), t1_raw[0], nc.scalar.copy, 0, SPLIT)
+        interleave("t1", t1_rows, 0, nc.scalar.copy, 0, SCALAR_FIRST_T1)
         for g in range(1, GROUPS):
-            interleave(("t1", g), t1_raw[g], nc.scalar.copy)
-        nc.scalar.activation(out=rho_f32[:], in_=rho_raw[:], func=ACT.Copy)
+            interleave("t1", t1_rows, g, nc.scalar.copy)
+        nc.scalar.activation(out=rho_f32[:], in_=rho_bf16[:], func=ACT.Copy)
 
-        interleave(("t1", 0), t1_raw[0], nc.vector.tensor_copy, SPLIT, B)
-        quantize_operand("t1", 0)
-        sort_words(0, 1)
-        group_pass("t1", 0, 0)
-        group_pass("t1", 1, 0)
-        for g in range(1, GROUPS):
-            sort_words(g, 0)
-            sort_words(g, 1)
-            quantize_operand("t1", g)
-            group_pass("t1", 0, g)
-            group_pass("t1", 1, g)
+        interleave("t1", t1_rows, 0, nc.vector.tensor_copy, SCALAR_FIRST_T1, B)
+        quantize("t1", 0)
+        sort_words_of_pass(0, 1)
         for g in range(GROUPS):
-            sort_words(g, 2)
+            if g > 0:
+                for o in range(EARLY):
+                    sort_words_of_pass(g, o)
+                quantize("t1", g)
+            for o in range(EARLY):
+                group_pass("t1", o, g)
 
-        for t in range(PACK):
-            recurrence(0, t)
-            whole_tile("t1", 2, t)
-        interleave(("z", 0), z_rows[0], nc.scalar.copy)
-        for g in range(GROUPS):
-            sort_words(g, 3)
-        for t in range(PACK):
-            recurrence(1, t)
-            whole_tile("t1", 3, t)
-        interleave(("z", 1), z_rows[1], nc.scalar.copy)
-        quantize_operand("z", 0)
-        for t in range(PACK):
+        for o in range(EARLY, GROUPS):
+            for pair in ((0, 1), (2, 3)):
+                first = (o, pair) == (EARLY, (0, 1))
+                if first:
+                    for t in pair:
+                        sort_words_of_slot(o, t)
+                for t in pair:
+                    recurrence(o - EARLY, t)
+                if pair[-1] == SLOTS - 1:
+                    interleave("z", z_rows, o - EARLY, nc.scalar.copy)
+                for t in pair:
+                    if not first:
+                        sort_words_of_slot(o, t)
+                    whole_tile("t1", o, t)
+
+        quantize("z", 0)
+        for t in range(SLOTS):
             recurrence(2, t)
-        interleave(("z", 2), z_rows[2], nc.scalar.copy)
+        interleave("z", z_rows, 2, nc.scalar.copy)
         group_pass("z", 0, 0)
-        quantize_operand("z", 1)
+        quantize("z", 1)
         group_pass("z", 0, 1)
-        for t in range(PACK):
+        for t in range(SLOTS):
             recurrence(3, t)
-        interleave(("z", 3), z_rows[3], nc.scalar.copy)
+        interleave("z", z_rows, 3, nc.scalar.copy, 0, SCALAR_LAST_Z)
         group_pass("z", 1, 0)
         group_pass("z", 1, 1)
+        interleave("z", z_rows, 3, nc.vector.tensor_copy, SCALAR_LAST_Z, B)
         for g in (2, 3):
-            quantize_operand("z", g)
+            quantize("z", g)
             group_pass("z", 0, g)
             group_pass("z", 1, g)
 
-        y_rows = [new("y_rows%d" % o, [P, PACK, B], F32) for o in range(GROUPS)]
-        y_codes = [new("y_codes%d" % o, [P, B], U32) for o in range(GROUPS)]
-        y_planes = new("y_planes", [P, B], U8)
-
-        def weigh(o, t, c0=0, c1=B):
-            nc.scalar.activation(
-                out=y_rows[o][:, t, c0:c1], in_=acc["z", o, t][:, c0:c1], func=ACT.Copy, scale=rho_f32[:, o, t : t + 1]
-            )
-
-        def out_rows(o):
-            return out_0[GROUP * o : GROUP * (o + 1), :].rearrange("(p t) b -> p t b", t=PACK)
-
-        def store_codes(o, c0, c1):
-            nc.sync.dma_start(
-                out=out_1[o].rearrange("p m t -> p (m t)").bitcast(I32)[:, c0:c1], in_=y_codes[o][:, c0:c1].bitcast(I32)
-            )
-
         last = GROUPS - 1
-        chunks = [(c0, c0 + P) for c0 in range(0, B, P)]
-        chunk_acc = []
-
-        def last_tile():
-            for c, (c0, c1) in enumerate(chunks):
-                bank = psum.tile([P, P], F32, name="bank%d" % ((BANKS - 1 + c) % BANKS))
-                chunk_acc.append(bank)
-                for g in range(GROUPS):
-                    codes, plane = operand["z", g]
-                    nc.tensor.matmul_mx(
-                        out=bank[:],
-                        lhsT=w_codes[g, last][:, 2 * P * (PACK - 1) :].bitcast(FP4X4),
-                        lhsT_scale=w_plane[g, last][:, P * (PACK - 1) :],
-                        rhs=codes[:, c0:c1].bitcast(FP8X4),
-                        rhs_scale=plane[:, c0:c1],
-                        start=(g == 0),
-                        stop=(g == GROUPS - 1),
-                    )
-
         for o in range(last):
-            for t in range(PACK):
-                weigh(o, t)
-                if o + 2 < GROUPS and (o + 2, t) != (last, PACK - 1):
-                    whole_tile("z", o + 2, t)
-            nc.sync.dma_start(out=out_rows(o), in_=y_rows[o][:])
-            interleave(("y", o), y_rows[o], nc.vector.tensor_copy)
-            quantize(("y", o), y_codes[o][:], y_planes[4 * o :, :])
-            store_codes(o, 0, B)
-        last_tile()
-        for t in range(PACK - 1):
-            weigh(last, t)
-            if t > 0:
-                t_from = 0 if t == 1 else t
-                nc.sync.dma_start(out=out_rows(last)[:, t_from : t + 1, :], in_=y_rows[last][:, t_from : t + 1, :])
+            for t in range(SLOTS):
+                weigh(sums["z", o, t], o, t)
+                store_rows(o, t)
+                if o + EARLY < GROUPS and (o + EARLY, t) != (last, SLOTS - 1):
+                    whole_tile("z", o + EARLY, t)
+            if o > 0:
+                store_codes(o - 1)
+            interleave("y", y_rows, o, nc.vector.tensor_copy)
+            quantize("y", o)
+
+        chunks = [(c0, c0 + P) for c0 in range(0, B, P)]
+        chunk_sums = []
         for c, (c0, c1) in enumerate(chunks):
-            nc.scalar.activation(
-                out=y_rows[last][:, PACK - 1, c0:c1], in_=chunk_acc[c][:], func=ACT.Copy,
-                scale=rho_f32[:, last, PACK - 1 : PACK],
-            )
-            if c == len(chunks) - 1:
-                nc.sync.dma_start(out=out_rows(last)[:, PACK - 1, :], in_=y_rows[last][:, PACK - 1, :])
-            interleave(("y", last), y_rows[last], nc.scalar.copy if c == len(chunks) - 1 else nc.vector.tensor_copy, c0, c1)
+            chunk_sums.append(bank_tile(BANKS - 1 + c, P))
+            for g in range(GROUPS):
+                one_pass(chunk_sums[c], "z", last, SLOTS - 1, g, c0, c1)
+        for t in range(SLOTS - 1):
+            weigh(sums["z", last, t], last, t)
+            if t == SLOTS - 2:
+                store_codes(last - 1)
+            store_rows(last, t)
+        for c, (c0, c1) in enumerate(chunks):
+            weigh(chunk_sums[c], last, SLOTS - 1, c0, c1)
+            if c < len(chunks) - 1:
+                interleave("y", y_rows, last, nc.vector.tensor_copy, c0, c1)
+            else:
+                store_rows(last, SLOTS - 1)
+                interleave("y", y_rows, last, nc.scalar.copy, c0, c1)
             if c > 0:
-                quantize(("y", last), y_codes[last][:], y_planes[4 * last :, :], c0 - P, c0)
-        quantize(("y", last), y_codes[last][:], y_planes[4 * last :, :], B - P, B)
-        store_codes(last, 0, B)
-        for q in range(4):
+                quantize("y", last, *chunks[c - 1])
+        quantize("y", last, *chunks[-1])
+        store_codes(last)
+        for q in range(QUADS):
             queue = nc.scalar if q % 2 == 0 else nc.sync
             queue.dma_start(
                 out=out_2[:, 4 * q : 4 * q + 4, :].bitcast(I32), in_=y_planes[32 * q : 32 * q + 16, :].bitcast(I32)

@@ -25,7 +25,6 @@ QUADS = 4
 ALIGN = 256
 EARLY = BANKS // SLOTS
 SCALAR_FIRST_T1 = 192
-SCALAR_LAST_Z = 256
 
 
 def tile_chebyshev_step_operator_apply_h1_kernel(tc, w_words, w_scales, t0, t1, rho, out_0, out_1, out_2):
@@ -45,7 +44,7 @@ def tile_chebyshev_step_operator_apply_h1_kernel(tc, w_words, w_scales, t0, t1, 
             nc.vector.memset(tile[:].bitcast(I32), 0)
 
         def load_scales():
-            for q in (0, 2, 1, 3):
+            for q in range(QUADS):
                 nc.sync.dma_start(
                     out=scales_raw[32 * q : 32 * q + 16, :].bitcast(I32),
                     in_=w_scales[:, 4 * q : 4 * q + 4, :].bitcast(I32),
@@ -74,9 +73,9 @@ def tile_chebyshev_step_operator_apply_h1_kernel(tc, w_words, w_scales, t0, t1, 
             columns = w_words[:, :, GROUP * WORD * o : GROUP * WORD * (o + 1)]
             nc.sync.dma_start(out=w_late[o][:].bitcast(I32), in_=columns.bitcast(I32).rearrange("g p n -> p g n"))
 
-        def sort_words_of_pass(g, o):
-            dst = new("w_pass%d_%d" % (g, o), [P, GROUP * WORD], U8)
-            src = w_early[g][:, GROUP * WORD * o : GROUP * WORD * (o + 1)]
+        def sort_words(g, o):
+            src = w_early[g][:, GROUP * WORD * o : GROUP * WORD * (o + 1)] if o < EARLY else w_late[o][:, g, :]
+            dst = new("w_sorted%d_%d" % (o, g), [P, GROUP * WORD], U8)
             nc.vector.tensor_copy(
                 out=dst[:].rearrange("p (t m y) -> p t m y", t=SLOTS, y=WORD),
                 in_=src.rearrange("p (m t y) -> p t m y", t=SLOTS, y=WORD),
@@ -84,19 +83,8 @@ def tile_chebyshev_step_operator_apply_h1_kernel(tc, w_words, w_scales, t0, t1, 
             for t in range(SLOTS):
                 w_tile[g, o, t] = dst[:, P * WORD * t : P * WORD * (t + 1)]
 
-        def sort_words_of_slot(o, t):
-            dst = new("w_slot%d_%d" % (o, t), [P, GROUPS, P * WORD], U8)
-            nc.vector.tensor_copy(
-                out=dst[:].rearrange("p g (m y) -> p g m y", y=WORD),
-                in_=w_late[o][:].rearrange("p g (m t y) -> p g m t y", t=SLOTS, y=WORD)[:, :, :, t, :],
-            )
-            for g in range(GROUPS):
-                w_tile[g, o, t] = dst[:, g, :]
-
         t1_rows = [new("t1_rows%d" % g, [P, SLOTS, B], BF16) for g in range(GROUPS)]
         t0_rows = [new("t0_rows%d" % g, [P, SLOTS, B], BF16) for g in range(GROUPS)]
-        z_rows = [new("z_rows%d" % g, [P, SLOTS, B], BF16) for g in range(GROUPS)]
-        y_rows = [new("y_rows%d" % g, [P, SLOTS, B], F32) for g in range(GROUPS)]
         rho_bf16 = new("rho_bf16", [P, GROUPS, SLOTS], BF16)
         rho_f32 = new("rho_f32", [P, GROUPS, SLOTS], F32)
 
@@ -121,10 +109,7 @@ def tile_chebyshev_step_operator_apply_h1_kernel(tc, w_words, w_scales, t0, t1, 
             for g in range(GROUPS):
                 codes[name, g] = new("%s_codes%d" % (name, g), [P, B], U32)
                 plane[name, g] = new("%s_plane%d" % (name, g), [P, B], U8)[:]
-        y_planes = new("y_planes", [P, B], U8)
-        for g in range(GROUPS):
-            codes["y", g] = new("y_codes%d" % g, [P, B], U32)
-            plane["y", g] = y_planes[4 * g :, :]
+        z_rows = [new("z_rows%d" % g, [P, SLOTS, B], BF16) for g in range(GROUPS)]
 
         def quantize(name, g, c0=0, c1=B):
             nc.vector.quantize_mx(
@@ -166,67 +151,51 @@ def tile_chebyshev_step_operator_apply_h1_kernel(tc, w_words, w_scales, t0, t1, 
                 op0=ALU.mult, op1=ALU.subtract,
             )
 
-        def weigh(src, o, t, c0=0, c1=B):
-            nc.scalar.activation(out=y_rows[o][:, t, c0:c1], in_=src[:], func=ACT.Copy, scale=rho_f32[:, o, t : t + 1])
-
-        def store_rows(o, t):
-            nc.sync.dma_start(out=group_rows(out_0, o)[:, t, :], in_=y_rows[o][:, t, :])
-
-        def store_codes(o):
-            nc.sync.dma_start(out=out_1[o].rearrange("p m t -> p (m t)").bitcast(I32), in_=codes["y", o][:].bitcast(I32))
-
         load_w_early(0)
         load_scales()
         load_rows(t1_rows, t1, 0)
         load_rows(t1_rows, t1, 1)
         load_w_early(1)
         load_rows(t1_rows, t1, 2)
-        load_w_early(2)
-        sort_words_of_pass(0, 0)
+        sort_words(0, 0)
         sort_scales()
         move_scales(1)
+        load_w_early(2)
         load_rows(t1_rows, t1, 3)
-        load_w_early(3)
         move_scales(2)
-        load_w_late(2)
+        load_w_early(3)
         move_scales(3)
+        load_w_late(2)
         load_rows(t0_rows, t0, 0)
         load_w_late(3)
-        load_rows(t0_rows, t0, 1)
         nc.sync.dma_start(out=rho_bf16[:], in_=rho.rearrange("(g p t) -> p g t", p=P, t=SLOTS))
-        load_rows(t0_rows, t0, 2)
-        load_rows(t0_rows, t0, 3)
+        for g in range(1, GROUPS):
+            load_rows(t0_rows, t0, g)
 
         interleave("t1", t1_rows, 0, nc.scalar.copy, 0, SCALAR_FIRST_T1)
         for g in range(1, GROUPS):
             interleave("t1", t1_rows, g, nc.scalar.copy)
-        nc.scalar.activation(out=rho_f32[:], in_=rho_bf16[:], func=ACT.Copy)
 
         interleave("t1", t1_rows, 0, nc.vector.tensor_copy, SCALAR_FIRST_T1, B)
         quantize("t1", 0)
-        sort_words_of_pass(0, 1)
+        sort_words(0, 1)
         for g in range(GROUPS):
             if g > 0:
                 for o in range(EARLY):
-                    sort_words_of_pass(g, o)
+                    sort_words(g, o)
                 quantize("t1", g)
             for o in range(EARLY):
                 group_pass("t1", o, g)
 
         for o in range(EARLY, GROUPS):
-            for pair in ((0, 1), (2, 3)):
-                first = (o, pair) == (EARLY, (0, 1))
-                if first:
-                    for t in pair:
-                        sort_words_of_slot(o, t)
-                for t in pair:
-                    recurrence(o - EARLY, t)
-                if pair[-1] == SLOTS - 1:
-                    interleave("z", z_rows, o - EARLY, nc.scalar.copy)
-                for t in pair:
-                    if not first:
-                        sort_words_of_slot(o, t)
-                    whole_tile("t1", o, t)
+            for g in range(GROUPS):
+                sort_words(g, o)
+            for t in range(SLOTS):
+                recurrence(o - EARLY, t)
+                whole_tile("t1", o, t)
+            interleave("z", z_rows, o - EARLY, nc.scalar.copy)
+            if o == EARLY:
+                nc.scalar.activation(out=rho_f32[:], in_=rho_bf16[:], func=ACT.Copy)
 
         quantize("z", 0)
         for t in range(SLOTS):
@@ -237,20 +206,36 @@ def tile_chebyshev_step_operator_apply_h1_kernel(tc, w_words, w_scales, t0, t1, 
         group_pass("z", 0, 1)
         for t in range(SLOTS):
             recurrence(3, t)
-        interleave("z", z_rows, 3, nc.scalar.copy, 0, SCALAR_LAST_Z)
+        interleave("z", z_rows, 3, nc.scalar.copy)
         group_pass("z", 1, 0)
         group_pass("z", 1, 1)
-        interleave("z", z_rows, 3, nc.vector.tensor_copy, SCALAR_LAST_Z, B)
         for g in (2, 3):
             quantize("z", g)
             group_pass("z", 0, g)
             group_pass("z", 1, g)
 
+        y_rows = [new("y_rows%d" % g, [P, SLOTS, B], F32) for g in range(GROUPS)]
+        for g in range(GROUPS):
+            codes["y", g] = new("y_codes%d" % g, [P, B], U32)
+        y_planes = new("y_planes", [P, B], U8)
+        for g in range(GROUPS):
+            plane["y", g] = y_planes[4 * g :, :]
+
+        def weigh(src, o, t, c0=0, c1=B):
+            nc.scalar.activation(out=y_rows[o][:, t, c0:c1], in_=src[:], func=ACT.Copy, scale=rho_f32[:, o, t : t + 1])
+
+        def store_rows(o, t_from, t_to):
+            nc.sync.dma_start(out=group_rows(out_0, o)[:, t_from:t_to, :], in_=y_rows[o][:, t_from:t_to, :])
+
+        def store_codes(o):
+            nc.sync.dma_start(out=out_1[o].rearrange("p m t -> p (m t)").bitcast(I32), in_=codes["y", o][:].bitcast(I32))
+
         last = GROUPS - 1
         for o in range(last):
             for t in range(SLOTS):
                 weigh(sums["z", o, t], o, t)
-                store_rows(o, t)
+                if t % 2 == 1:
+                    store_rows(o, t - 1, t + 1)
                 if o + EARLY < GROUPS and (o + EARLY, t) != (last, SLOTS - 1):
                     whole_tile("z", o + EARLY, t)
             if o > 0:
@@ -266,15 +251,16 @@ def tile_chebyshev_step_operator_apply_h1_kernel(tc, w_words, w_scales, t0, t1, 
                 one_pass(chunk_sums[c], "z", last, SLOTS - 1, g, c0, c1)
         for t in range(SLOTS - 1):
             weigh(sums["z", last, t], last, t)
-            if t == SLOTS - 2:
-                store_codes(last - 1)
-            store_rows(last, t)
+            if t == 1:
+                store_rows(last, 0, 2)
+        store_codes(last - 1)
+        store_rows(last, 2, 3)
         for c, (c0, c1) in enumerate(chunks):
             weigh(chunk_sums[c], last, SLOTS - 1, c0, c1)
             if c < len(chunks) - 1:
                 interleave("y", y_rows, last, nc.vector.tensor_copy, c0, c1)
             else:
-                store_rows(last, SLOTS - 1)
+                store_rows(last, SLOTS - 1, SLOTS)
                 interleave("y", y_rows, last, nc.scalar.copy, c0, c1)
             if c > 0:
                 quantize("y", last, *chunks[c - 1])

@@ -25,6 +25,7 @@ QUADS = 4
 ALIGN = 256
 EARLY = BANKS // SLOTS
 SCALAR_FIRST_T1 = 192
+SCALAR_LATER_T1 = 448
 
 
 def tile_chebyshev_step_operator_apply_h1_kernel(tc, w_words, w_scales, t0, t1, rho, out_0, out_1, out_2):
@@ -164,8 +165,8 @@ def tile_chebyshev_step_operator_apply_h1_kernel(tc, w_words, w_scales, t0, t1, 
         load_rows(t1_rows, t1, 3)
         move_scales(2)
         load_w_early(3)
-        move_scales(3)
         load_w_late(2)
+        move_scales(3)
         load_rows(t0_rows, t0, 0)
         load_w_late(3)
         nc.sync.dma_start(out=rho_bf16[:], in_=rho.rearrange("(g p t) -> p g t", p=P, t=SLOTS))
@@ -174,15 +175,16 @@ def tile_chebyshev_step_operator_apply_h1_kernel(tc, w_words, w_scales, t0, t1, 
 
         interleave("t1", t1_rows, 0, nc.scalar.copy, 0, SCALAR_FIRST_T1)
         for g in range(1, GROUPS):
-            interleave("t1", t1_rows, g, nc.scalar.copy)
+            interleave("t1", t1_rows, g, nc.scalar.copy, 0, SCALAR_LATER_T1)
 
         interleave("t1", t1_rows, 0, nc.vector.tensor_copy, SCALAR_FIRST_T1, B)
         quantize("t1", 0)
         sort_words(0, 1)
         for g in range(GROUPS):
             if g > 0:
-                for o in range(EARLY):
-                    sort_words(g, o)
+                sort_words(g, 0)
+                interleave("t1", t1_rows, g, nc.vector.tensor_copy, SCALAR_LATER_T1, B)
+                sort_words(g, 1)
                 quantize("t1", g)
             for o in range(EARLY):
                 group_pass("t1", o, g)

from contextlib import ExitStack

import concourse.mybir as mybir

N, B = 2048, 512
FLOPS = 2 * 2 * N * N * B

F32 = mybir.dt.float32
BF16 = mybir.dt.bfloat16
I32 = mybir.dt.int32
U32 = mybir.dt.uint32
U8 = mybir.dt.uint8
FP8X4 = mybir.dt.float8_e4m3fn_x4
FP4X4 = mybir.dt.float4_e2m1fn_x4
ALU = mybir.AluOpType
ACT = mybir.ActivationFunctionType

P = 128
SLOTS = 4
GROUP = P * SLOTS
GROUPS = N // GROUP
BANKS = 8
WORD = 2
QUADS = 4
ALIGN = 256
EARLY = BANKS // SLOTS
SCALAR_FIRST_T1 = 192
SCALAR_LATER_T1 = 448


def tile_chebyshev_step_operator_apply_h1_kernel(tc, w_words, w_scales, t0, t1, rho, out_0, out_1, out_2):
    nc = tc.nc
    with ExitStack() as ctx:
        keep = ctx.enter_context(tc.tile_pool(name="keep", bufs=1))
        staging = ctx.enter_context(tc.tile_pool(name="staging", bufs=GROUPS))
        psum = ctx.enter_context(tc.psum_pool(name="psum", bufs=1))
        ctx.enter_context(tc.manual_schedule())

        def new(name, shape, dtype):
            return keep.tile(shape, dtype, name=name, align_bytes=ALIGN)

        scales_raw = new("scales_raw", [P, N], U8)
        w_plane = [new("w_plane%d" % g, [P, N], U8) for g in range(GROUPS)]
        for tile in [scales_raw] + w_plane[1:]:
            nc.vector.memset(tile[:].bitcast(I32), 0)

        def load_scales():
            for q in range(QUADS):
                nc.sync.dma_start(
                    out=scales_raw[32 * q : 32 * q + 16, :].bitcast(I32),
                    in_=w_scales[:, 4 * q : 4 * q + 4, :].bitcast(I32),
                )

        def sort_scales():
            nc.vector.tensor_copy(
                out=w_plane[0][:].rearrange("p (o t m) -> p o t m", o=GROUPS, t=SLOTS),
                in_=scales_raw[:].rearrange("p (o m t) -> p o t m", o=GROUPS, t=SLOTS),
            )

        def move_scales(g):
            for r in range(4):
                nc.sync.dma_start(
                    out=w_plane[g][r:P:32, :].bitcast(I32), in_=w_plane[0][4 * g + r : P : 32, :].bitcast(I32)
                )

        w_early = [new("w_early%d" % g, [P, EARLY * GROUP * WORD], U8) for g in range(GROUPS)]
        w_late = {o: new("w_late%d" % o, [P, GROUPS, GROUP * WORD], U8) for o in range(EARLY, GROUPS)}
        w_tile = {}

        def load_w_early(g):
            nc.sync.dma_start(out=w_early[g][:].bitcast(I32), in_=w_words[g][:, 0 : EARLY * GROUP * WORD].bitcast(I32))

        def load_w_late(o):
            columns = w_words[:, :, GROUP * WORD * o : GROUP * WORD * (o + 1)]
            nc.sync.dma_start(out=w_late[o][:].bitcast(I32), in_=columns.bitcast(I32).rearrange("g p n -> p g n"))

        def sort_words(g, o):
            src = w_early[g][:, GROUP * WORD * o : GROUP * WORD * (o + 1)] if o < EARLY else w_late[o][:, g, :]
            dst = new("w_sorted%d_%d" % (o, g), [P, GROUP * WORD], U8)
            nc.vector.tensor_copy(
                out=dst[:].rearrange("p (t m y) -> p t m y", t=SLOTS, y=WORD),
                in_=src.rearrange("p (m t y) -> p t m y", t=SLOTS, y=WORD),
            )
            for t in range(SLOTS):
                w_tile[g, o, t] = dst[:, P * WORD * t : P * WORD * (t + 1)]

        t1_rows = [new("t1_rows%d" % g, [P, SLOTS, B], BF16) for g in range(GROUPS)]
        t0_rows = [new("t0_rows%d" % g, [P, SLOTS, B], BF16) for g in range(GROUPS)]
        rho_bf16 = new("rho_bf16", [P, GROUPS, SLOTS], BF16)
        rho_f32 = new("rho_f32", [P, GROUPS, SLOTS], F32)

        def group_rows(matrix, g):
            return matrix[GROUP * g : GROUP * (g + 1), :].rearrange("(p t) b -> p t b", t=SLOTS)

        def load_rows(tiles, matrix, g):
            nc.sync.dma_start(out=tiles[g][:], in_=group_rows(matrix, g))

        interleaved = {}

        def interleave(name, rows, g, copy, c0=0, c1=B):
            if (name, g) not in interleaved:
                interleaved[name, g] = staging.tile([P, B, SLOTS], BF16, name="interleaved", align_bytes=ALIGN)
            copy(
                out=interleaved[name, g][:, c0:c1, :].rearrange("p (c i) t -> p c t i", i=4),
                in_=rows[g][:, :, c0:c1].rearrange("p t (c i) -> p c t i", i=4),
            )

        codes, plane = {}, {}
        for name in ("t1", "z"):
            for g in range(GROUPS):
                codes[name, g] = new("%s_codes%d" % (name, g), [P, B], U32)
                plane[name, g] = new("%s_plane%d" % (name, g), [P, B], U8)[:]
        z_rows = [new("z_rows%d" % g, [P, SLOTS, B], BF16) for g in range(GROUPS)]

        def quantize(name, g, c0=0, c1=B):
            nc.vector.quantize_mx(
                out=codes[name, g][:, c0:c1].bitcast(FP8X4),
                scales=plane[name, g][:, c0:c1],
                in_=interleaved[name, g][:, c0:c1, :].rearrange("p c t -> p (c t)"),
            )

        sums = {}

        def bank_tile(bank, columns):
            return psum.tile([P, columns], F32, name="bank%d" % (bank % BANKS))

        def one_pass(dst, name, o, t, g, c0=0, c1=B):
            nc.tensor.matmul_mx(
                out=dst[:],
                lhsT=w_tile[g, o, t].bitcast(FP4X4),
                lhsT_scale=w_plane[g][:, GROUP * o + P * t : GROUP * o + P * (t + 1)],
                rhs=codes[name, g][:, c0:c1].bitcast(FP8X4),
                rhs_scale=plane[name, g][:, c0:c1],
                start=(g == 0),
                stop=(g == GROUPS - 1),
            )

        def group_pass(name, o, g):
            for t in range(SLOTS):
                if g == 0:
                    sums[name, o, t] = bank_tile(SLOTS * o + t, B)
                one_pass(sums[name, o, t], name, o, t, g)

        def whole_tile(name, o, t):
            sums[name, o, t] = bank_tile(SLOTS * o + t, B)
            for g in range(GROUPS):
                one_pass(sums[name, o, t], name, o, t, g)

        def recurrence(o, t):
            nc.vector.scalar_tensor_tensor(
                out=z_rows[o][:, t, :], in0=sums["t1", o, t][:], scalar=2.0, in1=t0_rows[o][:, t, :],
                op0=ALU.mult, op1=ALU.subtract,
            )

        load_w_early(0)
        load_scales()
        load_rows(t1_rows, t1, 0)
        load_rows(t1_rows, t1, 1)
        load_w_early(1)
        load_rows(t1_rows, t1, 2)
        sort_words(0, 0)
        sort_scales()
        move_scales(1)
        load_w_early(2)
        load_rows(t1_rows, t1, 3)
        move_scales(2)
        load_w_early(3)
        load_w_late(2)
        move_scales(3)
        load_rows(t0_rows, t0, 0)
        load_w_late(3)
        nc.sync.dma_start(out=rho_bf16[:], in_=rho.rearrange("(g p t) -> p g t", p=P, t=SLOTS))
        for g in range(1, GROUPS):
            load_rows(t0_rows, t0, g)

        interleave("t1", t1_rows, 0, nc.scalar.copy, 0, SCALAR_FIRST_T1)
        for g in range(1, GROUPS):
            interleave("t1", t1_rows, g, nc.scalar.copy, 0, SCALAR_LATER_T1)

        interleave("t1", t1_rows, 0, nc.vector.tensor_copy, SCALAR_FIRST_T1, B)
        quantize("t1", 0)
        sort_words(0, 1)
        for g in range(GROUPS):
            if g > 0:
                sort_words(g, 0)
                interleave("t1", t1_rows, g, nc.vector.tensor_copy, SCALAR_LATER_T1, B)
                sort_words(g, 1)
                quantize("t1", g)
            for o in range(EARLY):
                group_pass("t1", o, g)

        for o in range(EARLY, GROUPS):
            for g in range(GROUPS):
                sort_words(g, o)
            for t in range(SLOTS):
                recurrence(o - EARLY, t)
                whole_tile("t1", o, t)
            interleave("z", z_rows, o - EARLY, nc.scalar.copy)
            if o == EARLY:
                nc.scalar.activation(out=rho_f32[:], in_=rho_bf16[:], func=ACT.Copy)

        quantize("z", 0)
        for t in range(SLOTS):
            recurrence(2, t)
        interleave("z", z_rows, 2, nc.scalar.copy)
        group_pass("z", 0, 0)
        quantize("z", 1)
        group_pass("z", 0, 1)
        for t in range(SLOTS):
            recurrence(3, t)
        interleave("z", z_rows, 3, nc.scalar.copy)
        group_pass("z", 1, 0)
        group_pass("z", 1, 1)
        for g in (2, 3):
            quantize("z", g)
            group_pass("z", 0, g)
            group_pass("z", 1, g)

        y_rows = [new("y_rows%d" % g, [P, SLOTS, B], F32) for g in range(GROUPS)]
        for g in range(GROUPS):
            codes["y", g] = new("y_codes%d" % g, [P, B], U32)
        y_planes = new("y_planes", [P, B], U8)
        for g in range(GROUPS):
            plane["y", g] = y_planes[4 * g :, :]

        def weigh(src, o, t, c0=0, c1=B):
            nc.scalar.activation(out=y_rows[o][:, t, c0:c1], in_=src[:], func=ACT.Copy, scale=rho_f32[:, o, t : t + 1])

        def store_rows(o, t_from, t_to):
            nc.sync.dma_start(out=group_rows(out_0, o)[:, t_from:t_to, :], in_=y_rows[o][:, t_from:t_to, :])

        def store_codes(o):
            nc.sync.dma_start(out=out_1[o].rearrange("p m t -> p (m t)").bitcast(I32), in_=codes["y", o][:].bitcast(I32))

        last = GROUPS - 1
        for o in range(last):
            for t in range(SLOTS):
                weigh(sums["z", o, t], o, t)
                if t % 2 == 1:
                    store_rows(o, t - 1, t + 1)
                if o + EARLY < GROUPS and (o + EARLY, t) != (last, SLOTS - 1):
                    whole_tile("z", o + EARLY, t)
            if o > 0:
                store_codes(o - 1)
            interleave("y", y_rows, o, nc.vector.tensor_copy)
            quantize("y", o)

        chunks = [(c0, c0 + P) for c0 in range(0, B, P)]
        chunk_sums = []
        for c, (c0, c1) in enumerate(chunks):
            chunk_sums.append(bank_tile(BANKS - 1 + c, P))
            for g in range(GROUPS):
                one_pass(chunk_sums[c], "z", last, SLOTS - 1, g, c0, c1)
        for t in range(SLOTS - 1):
            weigh(sums["z", last, t], last, t)
            if t == 1:
                store_rows(last, 0, 2)
        store_codes(last - 1)
        store_rows(last, 2, 3)
        for c, (c0, c1) in enumerate(chunks):
            weigh(chunk_sums[c], last, SLOTS - 1, c0, c1)
            if c < len(chunks) - 1:
                interleave("y", y_rows, last, nc.vector.tensor_copy, c0, c1)
            else:
                store_rows(last, SLOTS - 1, SLOTS)
                interleave("y", y_rows, last, nc.scalar.copy, c0, c1)
            if c > 0:
                quantize("y", last, *chunks[c - 1])
        quantize("y", last, *chunks[-1])
        store_codes(last)
        for q in range(QUADS):
            queue = nc.scalar if q % 2 == 0 else nc.sync
            queue.dma_start(
                out=out_2[:, 4 * q : 4 * q + 4, :].bitcast(I32), in_=y_planes[32 * q : 32 * q + 16, :].bitcast(I32)
            )
